import numpy as np
import ml_dtypes


def mxq(x, axis, fmt="e4m3"):
    dtype, down = {"e4m3": (ml_dtypes.float8_e4m3fn, 7), "e5m2": (ml_dtypes.float8_e5m2, 14)}[fmt]
    v = np.moveaxis(np.asarray(x, np.float32).astype(ml_dtypes.bfloat16).astype(np.float64), axis, -1)
    blocks = v.reshape(v.shape[:-1] + (-1, 32))
    amax = np.abs(blocks).max(-1, keepdims=True)
    byte = np.maximum(np.where(amax > 0, np.frexp(amax)[1] - 1 + 127, 0) - down, 1)
    scale = np.exp2(byte - 127.0)
    codes = (blocks / scale).astype(np.float32).astype(dtype).astype(np.float64)
    return np.moveaxis((codes * scale).reshape(v.shape), -1, axis)


WIDE = False


def mx_kscale(k):
    if not WIDE:
        return np.ones(k)
    levels = np.array([10, -10, 5, -5, 0])
    if k % 512:
        return np.exp2(np.random.permutation(np.resize(levels, k // 32))).repeat(32)
    a = np.empty((k // 512, 16))
    for p in range(k // 512):
        a[p, :8] = np.random.permutation(np.resize(levels, 8))
        for g in range(8):
            far = levels[np.abs(levels - a[p, g]) >= 10]
            a[p, g + 8] = far[np.random.randint(len(far))]
    return np.exp2(a.ravel()).repeat(32)


def f64(x):
    return np.asarray(x).astype(np.float64)


def striped(idx):
    return np.tile(idx.reshape(-1, 16).T, (8, 1)).astype(np.uint16)


def unstriped(offs):
    return offs[:16].T.reshape(-1).astype(np.int64)


def striped8(idx):
    return np.concatenate([x.reshape(-1, 16).T for x in idx]).astype(np.uint16)


def runs(offs, k):
    lists = np.stack([offs[16 * r : 16 * r + 16].T.reshape(-1) for r in range(8)]).astype(np.int64)
    return lists[np.arange(k) % 512 // 64]


def pack_weight(w):
    k, n = w.shape
    w = f64(np.asarray(w, np.float32).astype(ml_dtypes.bfloat16)).reshape(k // 32, 32, n)
    amax = np.abs(w).max(1)
    byte = np.clip(np.where(amax > 0, np.frexp(amax)[1] - 1 + 127 - 7, 1), 1, 254)
    scaled = (w * np.exp2(127.0 - byte)[:, None, :]).reshape(k, n).astype(np.float32)
    words = np.ascontiguousarray(scaled.reshape(k // 512, 128, 4, n).transpose(0, 1, 3, 2)).astype(ml_dtypes.float8_e4m3fn).view(np.uint8)
    return words, np.ascontiguousarray(byte.astype(np.uint8).reshape(k // 512, 16, n))


def unpack_weight(words, scales):
    g, p, n, _ = words.shape
    vals = np.ascontiguousarray(words).view(ml_dtypes.float8_e4m3fn).astype(np.float64) * np.repeat(np.exp2(scales.astype(np.float64) - 127.0), 8, axis=1)[..., None]
    return vals.transpose(0, 1, 3, 2).reshape(g * 512, n)


def relu(v):
    return np.maximum(v, 0.0)


def sigmoid(v):
    return 1.0 / (1.0 + np.exp(-np.maximum(v, -700.0)))

def planes(y):
    n, m = y.shape
    v = y.astype(np.float32).astype(ml_dtypes.bfloat16).astype(np.float64).reshape(n // 32, 32, m)
    top = np.abs(v).max(1)
    byte = np.clip(np.where(top > 0, np.frexp(top)[1] - 1 + 127 - 7, 1), 1, 254)
    codes = (v * np.exp2(127.0 - byte)[:, None, :]).reshape(n, m).astype(np.float32).astype(ml_dtypes.float8_e4m3fn).view(np.uint8)
    words = codes.reshape(n // 512, 128, 4, m).transpose(0, 1, 3, 2)
    return np.ascontiguousarray(words), np.ascontiguousarray(byte.astype(np.uint8).reshape(n // 512, 16, m))


K, T, S, H, C = 512, 2048, 512, 512, 512


def setup_inputs():
    n = np.random.standard_normal
    s = mx_kscale(K)[:, None]
    packed_xT = pack_weight(n((K, T)) * s)
    packed_w1 = pack_weight(n((K, H)) / np.sqrt(K) / s)
    return {
        "x_words": packed_xT[0],
        "x_scales": packed_xT[1],
        "w1_words": packed_w1[0],
        "w1_scales": packed_w1[1],
        "gs": (np.random.uniform(0.5, 1.5, (K, 1)) / s).astype(np.float32),
        "offs": striped(np.random.permutation(T)[:S]),
        "cand": striped(np.random.permutation(T)[:C]),
        "n1": striped8(np.stack([np.random.permutation(S) for _ in range(8)])),
        "n2": striped8(np.stack([np.random.permutation(S) for _ in range(8)])),
    }


def reference(x_words, x_scales, w1_words, w1_scales, gs, offs, cand, n1, n2):
    x_cand = unpack_weight(x_words, x_scales)[:, unstriped(cand)]
    xq = unpack_weight(x_words, x_scales)[:, unstriped(offs)]
    h = relu(unpack_weight(w1_words, w1_scales).T @ xq)
    z = f64(gs) * h
    s = 0.0625 * ((x_cand.T @ mxq(z, 0, "e4m3")))
    mx = np.maximum(s[np.arange(C)[:, None], runs(n1, C)], s[np.arange(C)[:, None], runs(n2, C)])
    out_0 = relu(s - mx) * sigmoid(mx)
    return (out_0,) + planes(out_0)

@@ -1,0 +1,229 @@
+from contextlib import ExitStack
+
+import concourse.mybir as mybir
+
+K, T, S, H, C = 512, 2048, 512, 512, 512
+FLOPS = 2 * K * H * S + 2 * K * C * S
+
+F32 = mybir.dt.float32
+BF16 = mybir.dt.bfloat16
+I32 = mybir.dt.int32
+U32 = mybir.dt.uint32
+U16 = mybir.dt.uint16
+U8 = mybir.dt.uint8
+FP8X4 = mybir.dt.float8_e4m3fn_x4
+ALU = mybir.AluOpType
+ACT = mybir.ActivationFunctionType
+
+P = 128
+PACK = 4
+GROUP = 16
+BLOCK = 128
+OUT_WIDTHS = (256, 128, 128)
+
+
+def tile_picked_candwin_none_po_kernel(
+    tc, x_words, x_scales, w1_words, w1_scales, gs, offs, cand, n1, n2, out_0, out_1, out_2
+):
+    nc = tc.nc
+    with ExitStack() as ctx:
+        lists = ctx.enter_context(tc.tile_pool(name="lists", bufs=1))
+        keep = ctx.enter_context(tc.tile_pool(name="keep", bufs=1))
+        psum = ctx.enter_context(tc.psum_pool(name="psum", bufs=1))
+
+        offs_t = lists.tile([P, S // GROUP], U16, name="offs_t")
+        cand_t = lists.tile([P, C // GROUP], U16, name="cand_t")
+        n1_t = lists.tile([P, S // GROUP], U16, name="n1_t")
+        n2_t = lists.tile([P, S // GROUP], U16, name="n2_t")
+
+        xw = keep.tile([P, T], U32, name="xw", align_bytes=64)
+        xs = keep.tile([P, T], U8, name="xs", align_bytes=64)
+        w1w_raw = keep.tile([P, H], U32, name="w1w_raw", align_bytes=64)
+        w1s_raw = keep.tile([P, H], U8, name="w1s_raw", tag="staging", align_bytes=64)
+        gs_t = keep.tile([P, PACK], F32, name="gs_t", align_bytes=64)
+
+        nc.vector.memset(xs[:].bitcast(I32), 0)
+        nc.gpsimd.memset(w1s_raw[:].bitcast(I32), 0)
+
+        def load_scale_rows(dst, src):
+            for q in range(4):
+                queue = nc.sync if q % 2 == 0 else nc.scalar
+                queue.dma_start(
+                    out=dst[32 * q : 32 * q + 4, :].bitcast(I32), in_=src[0, 4 * q : 4 * q + 4, :].bitcast(I32)
+                )
+
+        nc.sync.dma_start(offs_t[:], offs)
+        nc.sync.dma_start(cand_t[:], cand)
+        nc.sync.dma_start(out=w1w_raw[:].bitcast(I32), in_=w1_words[0].rearrange("p n t -> p (n t)").bitcast(I32))
+        load_scale_rows(xs, x_scales)
+        nc.sync.dma_start(out=xw[:].bitcast(I32), in_=x_words[0].rearrange("p n t -> p (n t)").bitcast(I32))
+        load_scale_rows(w1s_raw, w1_scales)
+        nc.sync.dma_start(out=gs_t[:], in_=gs.rearrange("(p t) o -> p (t o)", t=PACK))
+        nc.sync.dma_start(n1_t[:], n1)
+        nc.sync.dma_start(n2_t[:], n2)
+
+        qw = keep.tile([P, S], U32, name="qw", align_bytes=64)
+        qs = keep.tile([P, S], U8, name="qs", align_bytes=64)
+        w1w = keep.tile([P, H], U32, name="w1w", align_bytes=64)
+        w1s = keep.tile([P, H], U8, name="w1s", align_bytes=64)
+        cw = keep.tile([P, C], U32, name="cw", align_bytes=64)
+        cs = keep.tile([P, C], U8, name="cs", align_bytes=64)
+
+        def deal_words(dst, src):
+            nc.vector.tensor_copy(
+                out=dst[:].rearrange("p (t m) -> p m t", t=PACK), in_=src[:].rearrange("p (m t) -> p m t", t=PACK)
+            )
+
+        def deal_bytes(dst, src):
+            nc.vector.tensor_copy(
+                out=dst[:].rearrange("p (t m) -> p t m", t=PACK), in_=src[:].rearrange("p (m t) -> p t m", t=PACK)
+            )
+
+        cs_raw = keep.tile([P, C], U8, name="cs_raw", align_bytes=64)
+        deal_words(w1w, w1w_raw)
+        nc.vector.tensor_copy(qs[:], xs[:].indirect(offs_t[:]))
+        nc.vector.tensor_copy(cs_raw[:], xs[:].indirect(cand_t[:]))
+        deal_bytes(cs, cs_raw)
+        half = S // 2
+        for u in range(2):
+            nc.vector.tensor_copy(
+                qw[:, u * half : (u + 1) * half],
+                xw[:].indirect(offs_t[:, u * half // GROUP : (u + 1) * half // GROUP]),
+            )
+        deal_bytes(w1s, w1s_raw)
+        cw_raw = keep.tile([P, C], U32, name="cw_raw", tag="staging", align_bytes=64)
+        nc.vector.tensor_copy(cw_raw[:], xw[:].indirect(cand_t[:]))
+        deal_words(cw, cw_raw)
+
+        n_blocks = S // BLOCK
+        h_ps = [psum.tile([P, PACK, BLOCK], F32, name="h_ps%d" % c) for c in range(n_blocks)]
+        s_ps = [psum.tile([P, S], F32, name="s_ps%d" % t) for t in range(PACK)]
+        s_sb = [keep.tile([P, S], F32, name="s_sb%d" % t, align_bytes=64) for t in range(PACK)]
+        zb = [keep.tile([P, BLOCK, PACK], BF16, name="zb%d" % c, align_bytes=64) for c in range(n_blocks)]
+        zw = [keep.tile([P, BLOCK], U32, name="zw%d" % c, align_bytes=64) for c in range(n_blocks)]
+        zs = [keep.tile([P, BLOCK], U8, name="zs%d" % c, align_bytes=64) for c in range(n_blocks)]
+
+        for c in range(n_blocks):
+            cols = slice(c * BLOCK, (c + 1) * BLOCK)
+            for t in range(PACK):
+                rows = slice(t * P, (t + 1) * P)
+                nc.tensor.matmul_mx(
+                    out=h_ps[c][:, t, :],
+                    lhsT=w1w[:, rows].bitcast(FP8X4),
+                    lhsT_scale=w1s[:, rows],
+                    rhs=qw[:, cols].bitcast(FP8X4),
+                    rhs_scale=qs[:, cols],
+                    start=True,
+                    stop=True,
+                )
+
+        def weigh(c):
+            nc.vector.scalar_tensor_tensor(
+                out=zb[c][:],
+                in0=h_ps[c][:].rearrange("p t n -> p n t"),
+                scalar=0.0,
+                in1=gs_t[:].unsqueeze(1).to_broadcast([P, BLOCK, PACK]),
+                op0=ALU.max,
+                op1=ALU.mult,
+            )
+
+        def score(c):
+            nc.vector.quantize_mx(
+                out=zw[c][:].bitcast(FP8X4), scales=zs[c][:], in_=zb[c][:].rearrange("p n t -> p (n t)")
+            )
+            cols = slice(c * BLOCK, (c + 1) * BLOCK)
+            for t in range(PACK):
+                rows = slice(t * P, (t + 1) * P)
+                nc.tensor.matmul_mx(
+                    out=s_ps[t][:, cols],
+                    lhsT=cw[:, rows].bitcast(FP8X4),
+                    lhsT_scale=cs[:, rows],
+                    rhs=zw[c][:].bitcast(FP8X4),
+                    rhs_scale=zs[c][:],
+                    start=True,
+                    stop=True,
+                )
+
+        def leave(t, cols):
+            nc.scalar.activation(out=s_sb[t][:, cols], in_=s_ps[t][:, cols], func=ACT.Copy, scale=0.0625)
+
+        weigh(0)
+        for c in range(n_blocks):
+            if c + 1 < n_blocks:
+                weigh(c + 1)
+            score(c)
+            if c == n_blocks - 2:
+                leave(0, slice(0, S - BLOCK))
+        leave(0, slice(S - BLOCK, S))
+        for t in range(1, PACK):
+            leave(t, slice(0, S))
+
+        yw = keep.tile([P, S], U32, name="yw", align_bytes=64)
+        ys = keep.tile([P, S], U8, name="ys", align_bytes=64)
+        out_rows = out_0.rearrange("(p t) j -> p t j", t=PACK)
+        words_out = out_1[0].rearrange("p n t -> p (n t)").bitcast(I32)
+
+        starts = [sum(OUT_WIDTHS[:i]) for i in range(len(OUT_WIDTHS))]
+        last = len(OUT_WIDTHS) - 1
+        work = []
+        for i, w in enumerate(OUT_WIDTHS):
+            work.append(
+                {
+                    key: keep.tile([P, PACK, w], F32, name="%s%d" % (key, i), align_bytes=64)
+                    for key in ("mx", "d", "sig", "y")
+                }
+            )
+            work[i]["yb"] = keep.tile([P, w, PACK], BF16, name="yb%d" % i, align_bytes=64)
+
+        def fetch(i):
+            w, j0, tl = OUT_WIDTHS[i], starts[i], work[i]
+            entries = slice(j0 // GROUP, (j0 + w) // GROUP)
+            for key in ("a", "b"):
+                tl[key] = keep.tile([P, PACK, w], F32, name="%s%d" % (key, i), tag=key, align_bytes=64)
+            for t in range(PACK):
+                nc.vector.tensor_copy(tl["a"][:, t, :], s_sb[t][:].indirect(n1_t[:, entries]))
+                nc.vector.tensor_copy(tl["b"][:, t, :], s_sb[t][:].indirect(n2_t[:, entries]))
+
+        def larger(i):
+            w, j0, tl = OUT_WIDTHS[i], starts[i], work[i]
+            nc.vector.tensor_tensor(out=tl["mx"][:], in0=tl["a"][:], in1=tl["b"][:], op=ALU.max)
+            nc.scalar.activation(out=tl["sig"][:], in_=tl["mx"][:], func=ACT.Sigmoid)
+            for t in range(PACK):
+                nc.vector.tensor_tensor(
+                    out=tl["d"][:, t, :], in0=s_sb[t][:, j0 : j0 + w], in1=tl["mx"][:, t, :], op=ALU.subtract
+                )
+
+        def finish(i):
+            w, j0, tl = OUT_WIDTHS[i], starts[i], work[i]
+            nc.vector.scalar_tensor_tensor(
+                out=tl["y"][:], in0=tl["d"][:], scalar=0.0, in1=tl["sig"][:], op0=ALU.max, op1=ALU.mult
+            )
+            nc.sync.dma_start(out=out_rows[:, :, j0 : j0 + w], in_=tl["y"][:])
+            if i == last:
+                nc.vector.tensor_copy(out=tl["yb"][:], in_=tl["y"][:].rearrange("p t n -> p n t"))
+            else:
+                nc.scalar.copy(out=tl["yb"][:], in_=tl["y"][:].rearrange("p t n -> p n t"))
+
+        def pack(i):
+            w, j0, tl = OUT_WIDTHS[i], starts[i], work[i]
+            nc.vector.quantize_mx(
+                out=yw[:, j0 : j0 + w].bitcast(FP8X4),
+                scales=ys[:, j0 : j0 + w],
+                in_=tl["yb"][:].rearrange("p n t -> p (n t)"),
+            )
+            nc.sync.dma_start(out=words_out[:, j0 : j0 + w], in_=yw[:, j0 : j0 + w].bitcast(I32))
+
+        for i in range(len(OUT_WIDTHS)):
+            fetch(i)
+            if i > 0:
+                finish(i - 1)
+            larger(i)
+            if i > 0:
+                pack(i - 1)
+        finish(last)
+        pack(last)
+        for q in range(4):
+            eng = nc.sync if q % 2 == 0 else nc.scalar
+            eng.dma_start(
+                out=out_2[0, 4 * q : 4 * q + 4, :].bitcast(I32), in_=ys[32 * q : 32 * q + 4, :].bitcast(I32)
+            )

@@ -19,7 +19,7 @@ P = 128
 PACK = 4
 GROUP = 16
 BLOCK = 128
-OUT_WIDTHS = (256, 128, 128)
+OUT_WIDTHS = (128, 128, 128, 128)
 
 
 def tile_picked_candwin_none_po_kernel(
@@ -45,19 +45,18 @@ def tile_picked_candwin_none_po_kernel(
         nc.vector.memset(xs[:].bitcast(I32), 0)
         nc.gpsimd.memset(w1s_raw[:].bitcast(I32), 0)
 
-        def load_scale_rows(dst, src):
+        def load_scale_rows(dst, src, queues):
             for q in range(4):
-                queue = nc.sync if q % 2 == 0 else nc.scalar
-                queue.dma_start(
+                queues[q % len(queues)].dma_start(
                     out=dst[32 * q : 32 * q + 4, :].bitcast(I32), in_=src[0, 4 * q : 4 * q + 4, :].bitcast(I32)
                 )
 
         nc.sync.dma_start(offs_t[:], offs)
         nc.sync.dma_start(cand_t[:], cand)
         nc.sync.dma_start(out=w1w_raw[:].bitcast(I32), in_=w1_words[0].rearrange("p n t -> p (n t)").bitcast(I32))
-        load_scale_rows(xs, x_scales)
+        load_scale_rows(xs, x_scales, (nc.sync, nc.scalar))
         nc.sync.dma_start(out=xw[:].bitcast(I32), in_=x_words[0].rearrange("p n t -> p (n t)").bitcast(I32))
-        load_scale_rows(w1s_raw, w1_scales)
+        load_scale_rows(w1s_raw, w1_scales, (nc.sync,))
         nc.sync.dma_start(out=gs_t[:], in_=gs.rearrange("(p t) o -> p (t o)", t=PACK))
         nc.sync.dma_start(n1_t[:], n1)
         nc.sync.dma_start(n2_t[:], n2)
@@ -179,7 +178,7 @@ def tile_picked_candwin_none_po_kernel(
             w, j0, tl = OUT_WIDTHS[i], starts[i], work[i]
             entries = slice(j0 // GROUP, (j0 + w) // GROUP)
             for key in ("a", "b"):
-                tl[key] = keep.tile([P, PACK, w], F32, name="%s%d" % (key, i), tag=key, align_bytes=64)
+                tl[key] = keep.tile([P, PACK, w], F32, name="%s%d" % (key, i), tag=key, bufs=2, align_bytes=64)
             for t in range(PACK):
                 nc.vector.tensor_copy(tl["a"][:, t, :], s_sb[t][:].indirect(n1_t[:, entries]))
                 nc.vector.tensor_copy(tl["b"][:, t, :], s_sb[t][:].indirect(n2_t[:, entries]))
@@ -188,8 +187,9 @@ def tile_picked_candwin_none_po_kernel(
             w, j0, tl = OUT_WIDTHS[i], starts[i], work[i]
             nc.vector.tensor_tensor(out=tl["mx"][:], in0=tl["a"][:], in1=tl["b"][:], op=ALU.max)
             nc.scalar.activation(out=tl["sig"][:], in_=tl["mx"][:], func=ACT.Sigmoid)
+            eng = nc.vector if i == last else nc.gpsimd
             for t in range(PACK):
-                nc.vector.tensor_tensor(
+                eng.tensor_tensor(
                     out=tl["d"][:, t, :], in0=s_sb[t][:, j0 : j0 + w], in1=tl["mx"][:, t, :], op=ALU.subtract
                 )
 

@@ -1,6 +1,7 @@
 from contextlib import ExitStack
 
 import concourse.mybir as mybir
+from concourse.masks import make_identity
 
 K, T, S, H, C = 512, 2048, 512, 512, 512
 FLOPS = 2 * K * H * S + 2 * K * C * S
@@ -19,7 +20,8 @@ P = 128
 PACK = 4
 GROUP = 16
 BLOCK = 128
-OUT_WIDTHS = (128, 128, 128, 128)
+HALF = 256
+PAIR = 2
 
 
 def tile_picked_candwin_none_po_kernel(
@@ -44,6 +46,8 @@ def tile_picked_candwin_none_po_kernel(
 
         nc.vector.memset(xs[:].bitcast(I32), 0)
         nc.gpsimd.memset(w1s_raw[:].bitcast(I32), 0)
+        ident = keep.tile([P, P], F32, name="ident", align_bytes=64)
+        make_identity(nc, ident[:])
 
         def load_scale_rows(dst, src, queues):
             for q in range(4):
@@ -65,40 +69,46 @@ def tile_picked_candwin_none_po_kernel(
         qs = keep.tile([P, S], U8, name="qs", align_bytes=64)
         w1w = keep.tile([P, H], U32, name="w1w", align_bytes=64)
         w1s = keep.tile([P, H], U8, name="w1s", align_bytes=64)
-        cw = keep.tile([P, C], U32, name="cw", align_bytes=64)
-        cs = keep.tile([P, C], U8, name="cs", align_bytes=64)
 
         def deal_words(dst, src):
-            nc.vector.tensor_copy(
-                out=dst[:].rearrange("p (t m) -> p m t", t=PACK), in_=src[:].rearrange("p (m t) -> p m t", t=PACK)
-            )
+            nc.vector.tensor_copy(out=dst.rearrange("p t m -> p m t"), in_=src.rearrange("p t m -> p m t"))
 
         def deal_bytes(dst, src):
-            nc.vector.tensor_copy(
-                out=dst[:].rearrange("p (t m) -> p t m", t=PACK), in_=src[:].rearrange("p (m t) -> p t m", t=PACK)
-            )
+            nc.vector.tensor_copy(out=dst, in_=src)
+
+        def in_list_order(tile):
+            return tile[:].rearrange("p (m t) -> p t m", t=PACK)
+
+        def in_tile_order(tile):
+            return tile[:].rearrange("p (t m) -> p t m", m=P)
 
         cs_raw = keep.tile([P, C], U8, name="cs_raw", align_bytes=64)
-        deal_words(w1w, w1w_raw)
-        nc.vector.tensor_copy(qs[:], xs[:].indirect(offs_t[:]))
+        cw = {}
+        cs = {}
+
+        def deal_candidate_bytes(pair, tag):
+            cs[pair] = keep.tile([P, PAIR * P], U8, name="cs%d" % pair, tag=tag, align_bytes=64)
+            deal_bytes(in_tile_order(cs[pair]), in_list_order(cs_raw)[:, pair * PAIR : (pair + 1) * PAIR, :])
+
+        def deal_candidate_words(pair, tag):
+            cw[pair] = keep.tile([P, PAIR * P], U32, name="cw%d" % pair, tag=tag, align_bytes=64)
+            deal_words(in_tile_order(cw[pair]), in_list_order(cw_raw)[:, pair * PAIR : (pair + 1) * PAIR, :])
+
+        deal_words(in_tile_order(w1w), in_list_order(w1w_raw))
         nc.vector.tensor_copy(cs_raw[:], xs[:].indirect(cand_t[:]))
-        deal_bytes(cs, cs_raw)
-        half = S // 2
-        for u in range(2):
-            nc.vector.tensor_copy(
-                qw[:, u * half : (u + 1) * half],
-                xw[:].indirect(offs_t[:, u * half // GROUP : (u + 1) * half // GROUP]),
-            )
-        deal_bytes(w1s, w1s_raw)
+        nc.vector.tensor_copy(qs[:], xs[:].indirect(offs_t[:]))
+        deal_candidate_bytes(0, "cs0")
+        nc.vector.tensor_copy(qw[:], xw[:].indirect(offs_t[:]))
+        deal_bytes(in_tile_order(w1s), in_list_order(w1s_raw))
         cw_raw = keep.tile([P, C], U32, name="cw_raw", tag="staging", align_bytes=64)
         nc.vector.tensor_copy(cw_raw[:], xw[:].indirect(cand_t[:]))
-        deal_words(cw, cw_raw)
+        deal_candidate_words(0, "cw0")
 
         n_blocks = S // BLOCK
-        h_ps = [psum.tile([P, PACK, BLOCK], F32, name="h_ps%d" % c) for c in range(n_blocks)]
-        s_ps = [psum.tile([P, S], F32, name="s_ps%d" % t) for t in range(PACK)]
+        h_ps = [psum.tile([P, PACK, BLOCK], F32, name="h_ps%d" % c, tag="bank%d" % c) for c in range(n_blocks)]
+        s_ps = [psum.tile([P, S], F32, name="s_ps%d" % t, tag="bank%d" % (n_blocks + t)) for t in range(PACK)]
         s_sb = [keep.tile([P, S], F32, name="s_sb%d" % t, align_bytes=64) for t in range(PACK)]
-        zb = [keep.tile([P, BLOCK, PACK], BF16, name="zb%d" % c, align_bytes=64) for c in range(n_blocks)]
+        zb = [keep.tile([P, BLOCK, PACK], BF16, name="zb%d" % c, tag="zb%d" % c, align_bytes=64) for c in range(n_blocks)]
         zw = [keep.tile([P, BLOCK], U32, name="zw%d" % c, align_bytes=64) for c in range(n_blocks)]
         zs = [keep.tile([P, BLOCK], U8, name="zs%d" % c, align_bytes=64) for c in range(n_blocks)]
 
@@ -126,22 +136,22 @@ def tile_picked_candwin_none_po_kernel(
                 op1=ALU.mult,
             )
 
-        def score(c):
+        def quantise(c):
             nc.vector.quantize_mx(
                 out=zw[c][:].bitcast(FP8X4), scales=zs[c][:], in_=zb[c][:].rearrange("p n t -> p (n t)")
             )
-            cols = slice(c * BLOCK, (c + 1) * BLOCK)
-            for t in range(PACK):
-                rows = slice(t * P, (t + 1) * P)
-                nc.tensor.matmul_mx(
-                    out=s_ps[t][:, cols],
-                    lhsT=cw[:, rows].bitcast(FP8X4),
-                    lhsT_scale=cs[:, rows],
-                    rhs=zw[c][:].bitcast(FP8X4),
-                    rhs_scale=zs[c][:],
-                    start=True,
-                    stop=True,
-                )
+
+        def score(t, c):
+            rows = slice(t % PAIR * P, (t % PAIR + 1) * P)
+            nc.tensor.matmul_mx(
+                out=s_ps[t][:, c * BLOCK : (c + 1) * BLOCK],
+                lhsT=cw[t // PAIR][:, rows].bitcast(FP8X4),
+                lhsT_scale=cs[t // PAIR][:, rows],
+                rhs=zw[c][:].bitcast(FP8X4),
+                rhs_scale=zs[c][:],
+                start=True,
+                stop=True,
+            )
 
         def leave(t, cols):
             nc.scalar.activation(out=s_sb[t][:, cols], in_=s_ps[t][:, cols], func=ACT.Copy, scale=0.0625)
@@ -150,11 +160,19 @@ def tile_picked_candwin_none_po_kernel(
         for c in range(n_blocks):
             if c + 1 < n_blocks:
                 weigh(c + 1)
-            score(c)
+            quantise(c)
+            for t in range(PAIR):
+                score(t, c)
             if c == n_blocks - 2:
                 leave(0, slice(0, S - BLOCK))
         leave(0, slice(S - BLOCK, S))
-        for t in range(1, PACK):
+        leave(1, slice(0, S))
+
+        deal_candidate_bytes(1, "zb%d" % (n_blocks - 2))
+        deal_candidate_words(1, "zb%d" % (n_blocks - 1))
+        for t in range(PAIR, PACK):
+            for c in range(n_blocks):
+                score(t, c)
             leave(t, slice(0, S))
 
         yw = keep.tile([P, S], U32, name="yw", align_bytes=64)
@@ -162,66 +180,96 @@ def tile_picked_candwin_none_po_kernel(
         out_rows = out_0.rearrange("(p t) j -> p t j", t=PACK)
         words_out = out_1[0].rearrange("p n t -> p (n t)").bitcast(I32)
 
-        starts = [sum(OUT_WIDTHS[:i]) for i in range(len(OUT_WIDTHS))]
-        last = len(OUT_WIDTHS) - 1
+        n_units = 4
+        last = n_units - 1
         work = []
-        for i, w in enumerate(OUT_WIDTHS):
+        for i in range(n_units):
             work.append(
                 {
-                    key: keep.tile([P, PACK, w], F32, name="%s%d" % (key, i), align_bytes=64)
-                    for key in ("mx", "d", "sig", "y")
+                    key: keep.tile([P, PAIR, HALF], F32, name="%s%d" % (key, i), align_bytes=64)
+                    for key in ("d",)
                 }
             )
-            work[i]["yb"] = keep.tile([P, w, PACK], BF16, name="yb%d" % i, align_bytes=64)
+        y = [keep.tile([P, PACK, HALF], F32, name="y%d" % h, align_bytes=64) for h in range(2)]
+        yb = [keep.tile([P, HALF, PACK], BF16, name="yb%d" % h, align_bytes=64) for h in range(2)]
+        blocks = [(e, c) for e in range(PAIR) for c in range(HALF // P)]
 
         def fetch(i):
-            w, j0, tl = OUT_WIDTHS[i], starts[i], work[i]
-            entries = slice(j0 // GROUP, (j0 + w) // GROUP)
-            for key in ("a", "b"):
-                tl[key] = keep.tile([P, PACK, w], F32, name="%s%d" % (key, i), tag=key, bufs=2, align_bytes=64)
-            for t in range(PACK):
-                nc.vector.tensor_copy(tl["a"][:, t, :], s_sb[t][:].indirect(n1_t[:, entries]))
-                nc.vector.tensor_copy(tl["b"][:, t, :], s_sb[t][:].indirect(n2_t[:, entries]))
-
-        def larger(i):
-            w, j0, tl = OUT_WIDTHS[i], starts[i], work[i]
-            nc.vector.tensor_tensor(out=tl["mx"][:], in0=tl["a"][:], in1=tl["b"][:], op=ALU.max)
-            nc.scalar.activation(out=tl["sig"][:], in_=tl["mx"][:], func=ACT.Sigmoid)
-            eng = nc.vector if i == last else nc.gpsimd
-            for t in range(PACK):
-                eng.tensor_tensor(
-                    out=tl["d"][:, t, :], in0=s_sb[t][:, j0 : j0 + w], in1=tl["mx"][:, t, :], op=ALU.subtract
+            j0, t0, tl = i // 2 * HALF, i % 2 * PAIR, work[i]
+            entries = slice(j0 // GROUP, (j0 + HALF) // GROUP)
+            tl["a"] = keep.tile([P, PAIR, HALF], F32, name="a%d" % i, tag="a", bufs=2, align_bytes=64)
+            tl["b"] = keep.tile([P, PAIR, HALF], F32, name="b%d" % i, tag="b", bufs=2, align_bytes=64)
+            if i < last:
+                tl["turned"] = psum.tile([P, PAIR, HALF], F32, name="turned%d" % i, tag="bank%d" % i)
+                for n, (e, c) in enumerate(blocks):
+                    nc.tensor.matmul(
+                        tl["turned"][:, e, c * P : (c + 1) * P], s_sb[t0 + e][:, j0 + c * P : j0 + (c + 1) * P], ident[:],
+                        start=(n == 0), stop=False, is_transpose=True,
+                    )
+            for e in range(PAIR):
+                nc.vector.tensor_copy(tl["a"][:, e, :], s_sb[t0 + e][:].indirect(n1_t[:, entries]))
+                nc.vector.tensor_scalar(
+                    tl["b"][:, e, :], s_sb[t0 + e][:].indirect(n2_t[:, entries]), -1.0, 0.0, ALU.mult, ALU.add
                 )
 
-        def finish(i):
-            w, j0, tl = OUT_WIDTHS[i], starts[i], work[i]
+        def larger(i):
+            j0, t0, tl = i // 2 * HALF, i % 2 * PAIR, work[i]
+            tl["mx"] = keep.tile([P, PAIR, HALF], F32, name="mx%d" % i, tag="mx%d" % i, align_bytes=64)
             nc.vector.scalar_tensor_tensor(
-                out=tl["y"][:], in0=tl["d"][:], scalar=0.0, in1=tl["sig"][:], op0=ALU.max, op1=ALU.mult
+                out=tl["mx"][:], in0=tl["a"][:], scalar=-1.0, in1=tl["b"][:], op0=ALU.mult, op1=ALU.min
             )
-            nc.sync.dma_start(out=out_rows[:, :, j0 : j0 + w], in_=tl["y"][:])
-            if i == last:
-                nc.vector.tensor_copy(out=tl["yb"][:], in_=tl["y"][:].rearrange("p t n -> p n t"))
+            tl["sig"] = keep.tile([P, PAIR, HALF], F32, name="sig%d" % i, tag="mx2" if i == last else "sig%d" % i, align_bytes=64)
+            nc.scalar.activation(out=tl["sig"][:], in_=tl["mx"][:], func=ACT.Sigmoid, scale=-1.0)
+            if i < last:
+                for n, (e, c) in enumerate(blocks):
+                    nc.tensor.matmul(
+                        tl["turned"][:, e, c * P : (c + 1) * P], tl["mx"][:, e, c * P : (c + 1) * P], ident[:],
+                        start=False, stop=(n == len(blocks) - 1), is_transpose=True,
+                    )
+                nc.scalar.activation(out=tl["d"][:], in_=tl["turned"][:], func=ACT.Relu)
+                tl["back"] = psum.tile([P, PAIR, HALF], F32, name="back%d" % i, tag="bank%d" % (n_blocks + i))
+                for e, c in blocks:
+                    nc.tensor.transpose(
+                        tl["back"][:, e, c * P : (c + 1) * P], tl["d"][:, e, c * P : (c + 1) * P], ident[:]
+                    )
             else:
-                nc.scalar.copy(out=tl["yb"][:], in_=tl["y"][:].rearrange("p t n -> p n t"))
+                for e in range(PAIR):
+                    nc.vector.tensor_tensor(
+                        out=tl["d"][:, e, :], in0=s_sb[t0 + e][:, j0 : j0 + HALF], in1=tl["mx"][:, e, :], op=ALU.add
+                    )
 
-        def pack(i):
-            w, j0, tl = OUT_WIDTHS[i], starts[i], work[i]
+        def finish(i):
+            h, t0, tl = i // 2, i % 2 * PAIR, work[i]
+            dst = y[h][:, t0 : t0 + PAIR, :]
+            if i < last:
+                nc.vector.tensor_tensor(out=dst, in0=tl["back"][:], in1=tl["sig"][:], op=ALU.mult)
+            else:
+                nc.vector.scalar_tensor_tensor(
+                    out=dst, in0=tl["d"][:], scalar=0.0, in1=tl["sig"][:], op0=ALU.max, op1=ALU.mult
+                )
+            nc.sync.dma_start(out=out_rows[:, t0 : t0 + PAIR, h * HALF : (h + 1) * HALF], in_=dst)
+
+        def round_off(h, cols, copy):
+            copy(out=yb[h][:, cols, :], in_=y[h][:, :, cols].rearrange("p t n -> p n t"))
+
+        def pack(h):
+            cols = slice(h * HALF, (h + 1) * HALF)
             nc.vector.quantize_mx(
-                out=yw[:, j0 : j0 + w].bitcast(FP8X4),
-                scales=ys[:, j0 : j0 + w],
-                in_=tl["yb"][:].rearrange("p n t -> p (n t)"),
+                out=yw[:, cols].bitcast(FP8X4), scales=ys[:, cols], in_=yb[h][:].rearrange("p n t -> p (n t)")
             )
-            nc.sync.dma_start(out=words_out[:, j0 : j0 + w], in_=yw[:, j0 : j0 + w].bitcast(I32))
+            nc.sync.dma_start(out=words_out[:, cols], in_=yw[:, cols].bitcast(I32))
 
-        for i in range(len(OUT_WIDTHS)):
+        for i in range(n_units):
             fetch(i)
-            if i > 0:
-                finish(i - 1)
             larger(i)
             if i > 0:
-                pack(i - 1)
+                finish(i - 1)
+            if i == 2:
+                round_off(0, slice(0, HALF), nc.scalar.copy)
         finish(last)
-        pack(last)
+        round_off(1, slice(0, HALF), nc.vector.tensor_copy)
+        pack(0)
+        pack(1)
         for q in range(4):
             eng = nc.sync if q % 2 == 0 else nc.scalar
             eng.dma_start(

from contextlib import ExitStack

import concourse.mybir as mybir
from concourse.masks import make_identity

K, T, S, H, C = 512, 2048, 512, 512, 512
FLOPS = 2 * K * H * S + 2 * K * C * S

F32 = mybir.dt.float32
BF16 = mybir.dt.bfloat16
I32 = mybir.dt.int32
U32 = mybir.dt.uint32
U16 = mybir.dt.uint16
U8 = mybir.dt.uint8
FP8X4 = mybir.dt.float8_e4m3fn_x4
ALU = mybir.AluOpType
ACT = mybir.ActivationFunctionType

P = 128
PACK = 4
GROUP = 16
BLOCK = 128
HALF = 256
PAIR = 2


def tile_picked_candwin_none_po_kernel(
    tc, x_words, x_scales, w1_words, w1_scales, gs, offs, cand, n1, n2, out_0, out_1, out_2
):
    nc = tc.nc
    with ExitStack() as ctx:
        lists = ctx.enter_context(tc.tile_pool(name="lists", bufs=1))
        keep = ctx.enter_context(tc.tile_pool(name="keep", bufs=1))
        psum = ctx.enter_context(tc.psum_pool(name="psum", bufs=1))

        offs_t = lists.tile([P, S // GROUP], U16, name="offs_t")
        cand_t = lists.tile([P, C // GROUP], U16, name="cand_t")
        n1_t = lists.tile([P, S // GROUP], U16, name="n1_t")
        n2_t = lists.tile([P, S // GROUP], U16, name="n2_t")

        xw = keep.tile([P, T], U32, name="xw", align_bytes=64)
        xs = keep.tile([P, T], U8, name="xs", align_bytes=64)
        w1w_raw = keep.tile([P, H], U32, name="w1w_raw", align_bytes=64)
        w1s_raw = keep.tile([P, H], U8, name="w1s_raw", tag="staging", align_bytes=64)
        gs_t = keep.tile([P, PACK], F32, name="gs_t", align_bytes=64)

        nc.vector.memset(xs[:].bitcast(I32), 0)
        nc.gpsimd.memset(w1s_raw[:].bitcast(I32), 0)
        ident = keep.tile([P, P], F32, name="ident", align_bytes=64)
        make_identity(nc, ident[:])

        def load_scale_rows(dst, src, queues):
            for q in range(4):
                queues[q % len(queues)].dma_start(
                    out=dst[32 * q : 32 * q + 4, :].bitcast(I32), in_=src[0, 4 * q : 4 * q + 4, :].bitcast(I32)
                )

        nc.sync.dma_start(offs_t[:], offs)
        nc.sync.dma_start(cand_t[:], cand)
        nc.sync.dma_start(out=w1w_raw[:].bitcast(I32), in_=w1_words[0].rearrange("p n t -> p (n t)").bitcast(I32))
        load_scale_rows(xs, x_scales, (nc.sync, nc.scalar))
        nc.sync.dma_start(out=xw[:].bitcast(I32), in_=x_words[0].rearrange("p n t -> p (n t)").bitcast(I32))
        load_scale_rows(w1s_raw, w1_scales, (nc.sync,))
        nc.sync.dma_start(out=gs_t[:], in_=gs.rearrange("(p t) o -> p (t o)", t=PACK))
        nc.sync.dma_start(n1_t[:], n1)
        nc.sync.dma_start(n2_t[:], n2)

        qw = keep.tile([P, S], U32, name="qw", align_bytes=64)
        qs = keep.tile([P, S], U8, name="qs", align_bytes=64)
        w1w = keep.tile([P, H], U32, name="w1w", align_bytes=64)
        w1s = keep.tile([P, H], U8, name="w1s", align_bytes=64)

        def deal_words(dst, src):
            nc.vector.tensor_copy(out=dst.rearrange("p t m -> p m t"), in_=src.rearrange("p t m -> p m t"))

        def deal_bytes(dst, src):
            nc.vector.tensor_copy(out=dst, in_=src)

        def in_list_order(tile):
            return tile[:].rearrange("p (m t) -> p t m", t=PACK)

        def in_tile_order(tile):
            return tile[:].rearrange("p (t m) -> p t m", m=P)

        cs_raw = keep.tile([P, C], U8, name="cs_raw", align_bytes=64)
        cw = {}
        cs = {}

        def deal_candidate_bytes(pair, tag):
            cs[pair] = keep.tile([P, PAIR * P], U8, name="cs%d" % pair, tag=tag, align_bytes=64)
            deal_bytes(in_tile_order(cs[pair]), in_list_order(cs_raw)[:, pair * PAIR : (pair + 1) * PAIR, :])

        def deal_candidate_words(pair, tag):
            cw[pair] = keep.tile([P, PAIR * P], U32, name="cw%d" % pair, tag=tag, align_bytes=64)
            deal_words(in_tile_order(cw[pair]), in_list_order(cw_raw)[:, pair * PAIR : (pair + 1) * PAIR, :])

        deal_words(in_tile_order(w1w), in_list_order(w1w_raw))
        nc.vector.tensor_copy(cs_raw[:], xs[:].indirect(cand_t[:]))
        nc.vector.tensor_copy(qs[:], xs[:].indirect(offs_t[:]))
        deal_candidate_bytes(0, "cs0")
        nc.vector.tensor_copy(qw[:], xw[:].indirect(offs_t[:]))
        deal_bytes(in_tile_order(w1s), in_list_order(w1s_raw))
        cw_raw = keep.tile([P, C], U32, name="cw_raw", tag="staging", align_bytes=64)
        nc.vector.tensor_copy(cw_raw[:], xw[:].indirect(cand_t[:]))
        deal_candidate_words(0, "cw0")

        n_blocks = S // BLOCK
        h_ps = [psum.tile([P, PACK, BLOCK], F32, name="h_ps%d" % c, tag="bank%d" % c) for c in range(n_blocks)]
        s_ps = [psum.tile([P, S], F32, name="s_ps%d" % t, tag="bank%d" % (n_blocks + t)) for t in range(PACK)]
        s_sb = [keep.tile([P, S], F32, name="s_sb%d" % t, align_bytes=64) for t in range(PACK)]
        zb = [keep.tile([P, BLOCK, PACK], BF16, name="zb%d" % c, tag="zb%d" % c, align_bytes=64) for c in range(n_blocks)]
        zw = [keep.tile([P, BLOCK], U32, name="zw%d" % c, align_bytes=64) for c in range(n_blocks)]
        zs = [keep.tile([P, BLOCK], U8, name="zs%d" % c, align_bytes=64) for c in range(n_blocks)]

        for c in range(n_blocks):
            cols = slice(c * BLOCK, (c + 1) * BLOCK)
            for t in range(PACK):
                rows = slice(t * P, (t + 1) * P)
                nc.tensor.matmul_mx(
                    out=h_ps[c][:, t, :],
                    lhsT=w1w[:, rows].bitcast(FP8X4),
                    lhsT_scale=w1s[:, rows],
                    rhs=qw[:, cols].bitcast(FP8X4),
                    rhs_scale=qs[:, cols],
                    start=True,
                    stop=True,
                )

        def weigh(c):
            nc.vector.scalar_tensor_tensor(
                out=zb[c][:],
                in0=h_ps[c][:].rearrange("p t n -> p n t"),
                scalar=0.0,
                in1=gs_t[:].unsqueeze(1).to_broadcast([P, BLOCK, PACK]),
                op0=ALU.max,
                op1=ALU.mult,
            )

        def quantise(c):
            nc.vector.quantize_mx(
                out=zw[c][:].bitcast(FP8X4), scales=zs[c][:], in_=zb[c][:].rearrange("p n t -> p (n t)")
            )

        def score(t, c):
            rows = slice(t % PAIR * P, (t % PAIR + 1) * P)
            nc.tensor.matmul_mx(
                out=s_ps[t][:, c * BLOCK : (c + 1) * BLOCK],
                lhsT=cw[t // PAIR][:, rows].bitcast(FP8X4),
                lhsT_scale=cs[t // PAIR][:, rows],
                rhs=zw[c][:].bitcast(FP8X4),
                rhs_scale=zs[c][:],
                start=True,
                stop=True,
            )

        def leave(t, cols):
            nc.scalar.activation(out=s_sb[t][:, cols], in_=s_ps[t][:, cols], func=ACT.Copy, scale=0.0625)

        weigh(0)
        for c in range(n_blocks):
            if c + 1 < n_blocks:
                weigh(c + 1)
            quantise(c)
            for t in range(PAIR):
                score(t, c)
            if c == n_blocks - 2:
                leave(0, slice(0, S - BLOCK))
        leave(0, slice(S - BLOCK, S))
        leave(1, slice(0, S))

        deal_candidate_bytes(1, "zb%d" % (n_blocks - 2))
        deal_candidate_words(1, "zb%d" % (n_blocks - 1))
        for t in range(PAIR, PACK):
            for c in range(n_blocks):
                score(t, c)
            leave(t, slice(0, S))

        yw = keep.tile([P, S], U32, name="yw", align_bytes=64)
        ys = keep.tile([P, S], U8, name="ys", align_bytes=64)
        out_rows = out_0.rearrange("(p t) j -> p t j", t=PACK)
        words_out = out_1[0].rearrange("p n t -> p (n t)").bitcast(I32)

        n_units = 4
        last = n_units - 1
        work = []
        for i in range(n_units):
            work.append(
                {
                    key: keep.tile([P, PAIR, HALF], F32, name="%s%d" % (key, i), align_bytes=64)
                    for key in ("d",)
                }
            )
        y = [keep.tile([P, PACK, HALF], F32, name="y%d" % h, align_bytes=64) for h in range(2)]
        yb = [keep.tile([P, HALF, PACK], BF16, name="yb%d" % h, align_bytes=64) for h in range(2)]
        blocks = [(e, c) for e in range(PAIR) for c in range(HALF // P)]

        def fetch(i):
            j0, t0, tl = i // 2 * HALF, i % 2 * PAIR, work[i]
            entries = slice(j0 // GROUP, (j0 + HALF) // GROUP)
            tl["a"] = keep.tile([P, PAIR, HALF], F32, name="a%d" % i, tag="a", bufs=2, align_bytes=64)
            tl["b"] = keep.tile([P, PAIR, HALF], F32, name="b%d" % i, tag="b", bufs=2, align_bytes=64)
            if i < last:
                tl["turned"] = psum.tile([P, PAIR, HALF], F32, name="turned%d" % i, tag="bank%d" % i)
                for n, (e, c) in enumerate(blocks):
                    nc.tensor.matmul(
                        tl["turned"][:, e, c * P : (c + 1) * P], s_sb[t0 + e][:, j0 + c * P : j0 + (c + 1) * P], ident[:],
                        start=(n == 0), stop=False, is_transpose=True,
                    )
            for e in range(PAIR):
                nc.vector.tensor_copy(tl["a"][:, e, :], s_sb[t0 + e][:].indirect(n1_t[:, entries]))
                nc.vector.tensor_scalar(
                    tl["b"][:, e, :], s_sb[t0 + e][:].indirect(n2_t[:, entries]), -1.0, 0.0, ALU.mult, ALU.add
                )

        def larger(i):
            j0, t0, tl = i // 2 * HALF, i % 2 * PAIR, work[i]
            tl["mx"] = keep.tile([P, PAIR, HALF], F32, name="mx%d" % i, tag="mx%d" % i, align_bytes=64)
            nc.vector.scalar_tensor_tensor(
                out=tl["mx"][:], in0=tl["a"][:], scalar=-1.0, in1=tl["b"][:], op0=ALU.mult, op1=ALU.min
            )
            tl["sig"] = keep.tile([P, PAIR, HALF], F32, name="sig%d" % i, tag="mx2" if i == last else "sig%d" % i, align_bytes=64)
            nc.scalar.activation(out=tl["sig"][:], in_=tl["mx"][:], func=ACT.Sigmoid, scale=-1.0)
            if i < last:
                for n, (e, c) in enumerate(blocks):
                    nc.tensor.matmul(
                        tl["turned"][:, e, c * P : (c + 1) * P], tl["mx"][:, e, c * P : (c + 1) * P], ident[:],
                        start=False, stop=(n == len(blocks) - 1), is_transpose=True,
                    )
                nc.scalar.activation(out=tl["d"][:], in_=tl["turned"][:], func=ACT.Relu)
                tl["back"] = psum.tile([P, PAIR, HALF], F32, name="back%d" % i, tag="bank%d" % (n_blocks + i))
                for e, c in blocks:
                    nc.tensor.transpose(
                        tl["back"][:, e, c * P : (c + 1) * P], tl["d"][:, e, c * P : (c + 1) * P], ident[:]
                    )
            else:
                for e in range(PAIR):
                    nc.vector.tensor_tensor(
                        out=tl["d"][:, e, :], in0=s_sb[t0 + e][:, j0 : j0 + HALF], in1=tl["mx"][:, e, :], op=ALU.add
                    )

        def finish(i):
            h, t0, tl = i // 2, i % 2 * PAIR, work[i]
            dst = y[h][:, t0 : t0 + PAIR, :]
            if i < last:
                nc.vector.tensor_tensor(out=dst, in0=tl["back"][:], in1=tl["sig"][:], op=ALU.mult)
            else:
                nc.vector.scalar_tensor_tensor(
                    out=dst, in0=tl["d"][:], scalar=0.0, in1=tl["sig"][:], op0=ALU.max, op1=ALU.mult
                )
            nc.sync.dma_start(out=out_rows[:, t0 : t0 + PAIR, h * HALF : (h + 1) * HALF], in_=dst)

        def round_off(h, cols, copy):
            copy(out=yb[h][:, cols, :], in_=y[h][:, :, cols].rearrange("p t n -> p n t"))

        def pack(h):
            cols = slice(h * HALF, (h + 1) * HALF)
            nc.vector.quantize_mx(
                out=yw[:, cols].bitcast(FP8X4), scales=ys[:, cols], in_=yb[h][:].rearrange("p n t -> p (n t)")
            )
            nc.sync.dma_start(out=words_out[:, cols], in_=yw[:, cols].bitcast(I32))

        for i in range(n_units):
            fetch(i)
            larger(i)
            if i > 0:
                finish(i - 1)
            if i == 2:
                round_off(0, slice(0, HALF), nc.scalar.copy)
        finish(last)
        round_off(1, slice(0, HALF), nc.vector.tensor_copy)
        pack(0)
        pack(1)
        for q in range(4):
            eng = nc.sync if q % 2 == 0 else nc.scalar
            eng.dma_start(
                out=out_2[0, 4 * q : 4 * q + 4, :].bitcast(I32), in_=ys[32 * q : 32 * q + 4, :].bitcast(I32)
            )
